import numpy as np, ml_dtypes
CORES = [211,219,227,235,243,251,83,91,99,107,115,123]
N = 12
TK = 128
def setup_inputs(rng):
    return {"b": rng.standard_normal((N, 128, TK), dtype=np.float32).astype(ml_dtypes.bfloat16), "l": (rng.standard_normal((N, 128, N * 128), dtype=np.float32) / 16).astype(ml_dtypes.bfloat16)}
def setup_inputs_big(rng):
    d = setup_inputs(rng)
    for k in ("b",): d[k] = (d[k].astype(np.float32) * 1048576.0).astype(d[k].dtype)
    return d
def setup_inputs_small(rng):
    d = setup_inputs(rng)
    for k in ("b",): d[k] = (d[k].astype(np.float32) * (1 / 1048576.0)).astype(d[k].dtype)
    return d
def setup_inputs_apart(rng):
    d = setup_inputs(rng)
    f = (10.0 ** rng.permutation(np.linspace(-1.5, 1.5, N))).astype(np.float32).reshape(N, 1, 1)
    for k in ("b",): d[k] = (d[k].astype(np.float32) * f).astype(d[k].dtype)
    return d
def reference(b, l):
    B, L = b.astype(np.float64), l.astype(np.float64)
    y = np.zeros((N, 128, TK))
    for r in range(N):
        acc = B[r].copy()
        for s in range(r):
            acc -= L[r][:, 128 * s:128 * s + 128].T @ y[s]
        y[r] = acc
    return {"y": y.astype(ml_dtypes.bfloat16)}

@@ -1,0 +1,252 @@
+import comms_topo
+from concourse.bass import DstId, RemoteDMATransfer
+from concourse.mybir import AluOpType
+
+CORES = [211, 219, 227, 235, 243, 251, 83, 91, 99, 107, 115, 123]
+N = 12
+TW = 128
+GROUP_SIZES = (6, 6)
+PAIR = True
+
+
+def _bits(m):
+    n = 0
+    while m:
+        n += m & 1
+        m >>= 1
+    return n
+
+
+def build_plan(cores, topo):
+    n = len(cores)
+    grp, g0 = [], []
+    a = 0
+    for gi, sz in enumerate(GROUP_SIZES):
+        for _ in range(sz):
+            grp.append(gi)
+            g0.append(a)
+        a += sz
+    unit, duo = [None] * n, [None] * n
+    t = 0
+    while t < n:
+        pair = t + 1 < n and grp[t + 1] == grp[t] and topo.mates(cores[t], cores[t + 1])
+        duo[t] = t
+        unit[t] = (t,)
+        if pair:
+            duo[t + 1] = t
+            unit[t + 1] = (t + 1,)
+            if PAIR and grp[t] >= 1:
+                unit[t] = unit[t + 1] = (t, t + 1)
+            t += 1
+        t += 1
+
+    def seg_range(r, m):
+        if m == r:
+            return None
+        if m in unit[r]:
+            if m < r:
+                return (0, m + 1)
+            return (0, g0[m] + 1) if unit[r][-1] < n - 1 else None
+        if m > r:
+            return None
+        if grp[m] == 0:
+            return (0, m + 1)
+        return (g0[m] + 1, m + 1) if m > g0[m] else None
+
+    off, width = [], 0
+    for r in range(n):
+        o, d = 0, {}
+        for m in range(n):
+            rg = seg_range(r, m)
+            if rg:
+                d[m] = o
+                o += rg[1] - rg[0]
+        off.append(d)
+        width = max(width, o)
+
+    def ordered(m, dests):
+        later = [r for r in dests if grp[r] > grp[m]]
+        own = [r for r in dests if grp[r] == grp[m]]
+        return later + own
+
+    def mask_of(src, dests):
+        k = topo.mask(cores[src], cores[dests[0]])
+        for d in dests[1:]:
+            k &= topo.mask(cores[src], cores[d])
+        return k
+
+    rows_calls, p_calls = [], []
+    rw_inc = [dict() for _ in range(n)]
+    pa_inc = [dict() for _ in range(n)]
+    for m in range(n):
+        dests = [r for r in range(n) if seg_range(r, m)]
+        mates = [r for r in dests if r in unit[m]]
+        rest = ordered(m, [r for r in dests if r not in unit[m]])
+        calls = []
+        for r in mates + rest:
+            rg = seg_range(r, m)
+            if calls and calls[-1][0] == rg and duo[calls[-1][1][-1]] == duo[r]:
+                calls[-1][1].append(r)
+            else:
+                calls.append((rg, [r]))
+        calls = [(rg, ds, mask_of(m, ds)) for rg, ds in calls]
+        for rg, ds, k in calls:
+            for r in ds:
+                rw_inc[r][m] = _bits(k)
+        rows_calls.append(calls)
+        pc = []
+        if grp[m] >= 1:
+            u = unit[m]
+            mine = []
+            for r in range(u[-1] + 1, n):
+                srv = [q for q in u if topo.same_plane(cores[q], cores[r])]
+                if (srv[0] if srv else u[0]) == m:
+                    mine.append(r)
+            mine = ordered(m, mine)
+            for r in mine:
+                if pc and grp[pc[-1][-1]] == grp[r]:
+                    pc[-1].append(r)
+                else:
+                    pc.append([r])
+            pc = [(ds, mask_of(m, ds)) for ds in pc]
+            for ds, k in pc:
+                for r in ds:
+                    pa_inc[r][u[0]] = _bits(k)
+        p_calls.append(pc)
+    return dict(grp=grp, g0=g0, unit=unit, seg_range=seg_range, off=off, width=width,
+                rows_calls=rows_calls, p_calls=p_calls, rw_inc=rw_inc, pa_inc=pa_inc)
+
+
+SCRATCH = {
+    "lsb": ("sbuf", [128, (N + 1) * TW], "bfloat16"),
+    "seg": ("sbuf", [128, max(1, build_plan(CORES, comms_topo)["width"]) * TW], "bfloat16"),
+    "pb": ("sbuf", [128, N * TW], "bfloat16"),
+    "ysb": ("sbuf", [128, N * TW], "bfloat16"),
+    "c0": ("psum", [128, 512], "float32"),
+    "c1": ("psum", [128, 512], "float32"),
+    "a0": ("psum", [128, 512], "float32"),
+    "a1": ("psum", [128, 512], "float32"),
+}
+SEMAPHORES = ["ldl", "ldb", "st", "sent"] + [p + str(i) for p in ("rw", "pa", "mm", "vy", "am", "vp") for i in range(N)]
+
+
+def rank_program(g, core, T, topo):
+    r = T.rank_of(core)
+    if r is None:
+        return
+    cores = list(T.cores)
+    n = len(cores)
+    P = build_plan(cores, topo)
+    grp, g0, unit, seg_range, off = P["grp"], P["g0"], P["unit"], P["seg_range"], P["off"]
+    queues = {"g": g, "t": g.tensor, "v": g.vector, "s": g.sync}
+    waited = {"g": {}, "t": {}, "v": {}, "s": {}}
+
+    def need(q, sem, val):
+        if waited[q].get(sem, 0) < val:
+            queues[q].wait_ge(T.sem[sem], val)
+            waited[q][sem] = val
+
+    def cols(buf, k, w=1):
+        return buf[:, k * TW:(k + w) * TW]
+
+    def ext(m, e):
+        if m == r:
+            return (cols(T.lsb, e), "ldb" if e == 0 else "ldl", 16)
+        return (cols(T.seg, off[r][m] + e - seg_range(r, m)[0]), "rw%d" % m, P["rw_inc"][r][m])
+
+    def p_src(t):
+        if grp[t] == 0:
+            return ext(t, 0)
+        if t in unit[r]:
+            return (cols(T.pb, t), "vp%d" % t, 1)
+        return (cols(T.pb, t), "pa%d" % unit[t][0], P["pa_inc"][r][unit[t][0]])
+
+    def y_src(t):
+        if t == g0[t]:
+            return p_src(t)
+        return (cols(T.ysb, t), "vy%d" % t, 1)
+
+    if r >= 1:
+        g.sync.dma_start(T.lsb[:, TW:(r + 1) * TW], T.l[:, 0:r * TW]).then_inc(T.sem.ldl, 16)
+    g.scalar.dma_start(T.lsb[:, 0:TW], T.b[:, :]).then_inc(T.sem.ldb, 16)
+
+    sent = [0]
+
+    def send(src, dst_of, dests, mask, sem):
+        if len(dests) == 1:
+            rid, pid = topo.addr(cores[dests[0]], core)
+            g.remote_dma(dst_of(dests[0]), src, T.sem[sem], T.sem.sent, pid, rid, mask)
+        else:
+            ids = []
+            for d in dests:
+                rid, pid = topo.addr(cores[d], core)
+                ids.append(DstId(rid=rid, pnc=pid))
+            g.remote_dma_fused([RemoteDMATransfer(dst_ids=ids, dma_engine_mask=mask, remote_sem=T.sem[sem],
+                                                  srcs=[src], dsts=[dst_of(d) for d in dests], alu_op=0)],
+                               local_sem=T.sem.sent)
+        sent[0] += _bits(mask)
+
+    for (e0, e1), dests, mask in P["rows_calls"][r]:
+        if e0 == 0:
+            need("g", "ldb", 16)
+        if e1 > 1:
+            need("g", "ldl", 16)
+        send(cols(T.lsb, e0, e1 - e0), lambda d: cols(T.seg, off[d][r], e1 - e0), dests, mask, "rw%d" % r)
+
+    gr0 = g0[r]
+    has_dests = unit[r][-1] < n - 1
+    accrows = [m for m in unit[r] if m <= r or has_dests] if grp[r] >= 1 else []
+    accbank = [T.a0[:, 0:TW], T.a1[:, 0:TW]]
+    chain = [T.c0[:, 0:TW], T.c1[:, 0:TW]]
+    last_user = [None, None]
+    ci = 0
+    for t in range(r + 1):
+        G = g0[t]
+        if t > G:
+            bank = chain[ci % 2]
+            if last_user[ci % 2] is not None:
+                need("t", "vy%d" % last_user[ci % 2], 1)
+            last_user[ci % 2] = t
+            ci += 1
+            for s in range(G, t):
+                la, ls, lv = ext(t, 1 + s)
+                ya, ys, yv = y_src(s)
+                need("t", ls, lv)
+                need("t", ys, yv)
+                ins = g.tensor.matmul(bank, la, ya, s == G, s == t - 1)
+                if s == t - 1:
+                    ins.then_inc(T.sem["mm%d" % t], 1)
+            pa, ps, pv = p_src(t)
+            need("v", "mm%d" % t, 1)
+            need("v", ps, pv)
+            g.vector.tensor_tensor(cols(T.ysb, t), pa, bank, AluOpType.subtract).then_inc(T.sem["vy%d" % t], 1)
+        if 1 <= t <= gr0 and accrows:
+            s = t - 1
+            ya, ys, yv = y_src(s)
+            for i, m in enumerate(accrows):
+                la, ls, lv = ext(m, 1 + s)
+                need("t", ls, lv)
+                need("t", ys, yv)
+                ins = g.tensor.matmul(accbank[i], la, ya, s == 0, s == gr0 - 1)
+                if s == gr0 - 1:
+                    ins.then_inc(T.sem["am%d" % m], 1)
+            if t == gr0:
+                for i, m in enumerate(accrows):
+                    ba, bs, bv = ext(m, 0)
+                    need("v", "am%d" % m, 1)
+                    need("v", bs, bv)
+                    g.vector.tensor_tensor(cols(T.pb, m), ba, accbank[i], AluOpType.subtract).then_inc(
+                        T.sem["vp%d" % m], 1)
+
+    u = unit[r]
+    for dests, mask in P["p_calls"][r]:
+        for m in u:
+            need("g", "vp%d" % m, 1)
+        send(cols(T.pb, u[0], len(u)), lambda d: cols(T.pb, u[0], len(u)), dests, mask, "pa%d" % u[0])
+    if sent[0]:
+        g.wait_ge(T.sem.sent, sent[0])
+
+    ya, ys, yv = y_src(r)
+    need("s", ys, yv)
+    g.sync.dma_start(T.y[:, :], ya).then_inc(T.sem.st, 16)
+    g.sync.wait_ge(T.sem.st, 16)

@@ -5,8 +5,7 @@ from concourse.mybir import AluOpType
 CORES = [211, 219, 227, 235, 243, 251, 83, 91, 99, 107, 115, 123]
 N = 12
 TW = 128
-GROUP_SIZES = (6, 6)
-PAIR = True
+G = 6
 
 
 def _bits(m):
@@ -19,26 +18,20 @@ def _bits(m):
 
 def build_plan(cores, topo):
     n = len(cores)
-    grp, g0 = [], []
-    a = 0
-    for gi, sz in enumerate(GROUP_SIZES):
-        for _ in range(sz):
-            grp.append(gi)
-            g0.append(a)
-        a += sz
     unit, duo = [None] * n, [None] * n
     t = 0
     while t < n:
-        pair = t + 1 < n and grp[t + 1] == grp[t] and topo.mates(cores[t], cores[t + 1])
+        pair = t + 1 < n and (t < G) == (t + 1 < G) and topo.mates(cores[t], cores[t + 1])
         duo[t] = t
         unit[t] = (t,)
         if pair:
             duo[t + 1] = t
             unit[t + 1] = (t + 1,)
-            if PAIR and grp[t] >= 1:
+            if t >= G:
                 unit[t] = unit[t + 1] = (t, t + 1)
             t += 1
         t += 1
+    last = unit[n - 1]
 
     def seg_range(r, m):
         if m == r:
@@ -46,12 +39,12 @@ def build_plan(cores, topo):
         if m in unit[r]:
             if m < r:
                 return (0, m + 1)
-            return (0, g0[m] + 1) if unit[r][-1] < n - 1 else None
+            return (0, G + 1) if r not in last else None
         if m > r:
             return None
-        if grp[m] == 0:
-            return (0, m + 1)
-        return (g0[m] + 1, m + 1) if m > g0[m] else None
+        if m < G:
+            return None if (r in last and m > 0) else (0, m + 1)
+        return (G + 1, m + 1) if m > G else None
 
     off, width = [], 0
     for r in range(n):
@@ -64,26 +57,26 @@ def build_plan(cores, topo):
         off.append(d)
         width = max(width, o)
 
-    def ordered(m, dests):
-        later = [r for r in dests if grp[r] > grp[m]]
-        own = [r for r in dests if grp[r] == grp[m]]
-        return later + own
-
     def mask_of(src, dests):
         k = topo.mask(cores[src], cores[dests[0]])
         for d in dests[1:]:
             k &= topo.mask(cores[src], cores[d])
         return k
 
-    rows_calls, p_calls = [], []
+    rows_calls, p_calls, y_calls = [], [], []
     rw_inc = [dict() for _ in range(n)]
     pa_inc = [dict() for _ in range(n)]
+    ya_inc = [dict() for _ in range(n)]
     for m in range(n):
         dests = [r for r in range(n) if seg_range(r, m)]
-        mates = [r for r in dests if r in unit[m]]
-        rest = ordered(m, [r for r in dests if r not in unit[m]])
+        if m < G:
+            order = ([r for r in dests if r >= G and r not in last] + [r for r in dests if r < G]
+                     + [r for r in dests if r in last])
+        else:
+            order = (sorted([r for r in dests if r not in unit[m]], key=lambda r: (-duo[r], r))
+                     + [r for r in dests if r in unit[m]])
         calls = []
-        for r in mates + rest:
+        for r in order:
             rg = seg_range(r, m)
             if calls and calls[-1][0] == rg and duo[calls[-1][1][-1]] == duo[r]:
                 calls[-1][1].append(r)
@@ -95,39 +88,49 @@ def build_plan(cores, topo):
                 rw_inc[r][m] = _bits(k)
         rows_calls.append(calls)
         pc = []
-        if grp[m] >= 1:
+        if m >= G:
             u = unit[m]
             mine = []
-            for r in range(u[-1] + 1, n):
+            for r in range(n - 1, u[-1], -1):
                 srv = [q for q in u if topo.same_plane(cores[q], cores[r])]
                 if (srv[0] if srv else u[0]) == m:
                     mine.append(r)
-            mine = ordered(m, mine)
-            for r in mine:
-                if pc and grp[pc[-1][-1]] == grp[r]:
-                    pc[-1].append(r)
-                else:
-                    pc.append([r])
-            pc = [(ds, mask_of(m, ds)) for ds in pc]
-            for ds, k in pc:
-                for r in ds:
-                    pa_inc[r][u[0]] = _bits(k)
+            if mine:
+                pc = [(mine, mask_of(m, mine))]
+                for r in mine:
+                    pa_inc[r][u[0]] = _bits(pc[0][1])
         p_calls.append(pc)
-    return dict(grp=grp, g0=g0, unit=unit, seg_range=seg_range, off=off, width=width,
-                rows_calls=rows_calls, p_calls=p_calls, rw_inc=rw_inc, pa_inc=pa_inc)
+        yc = []
+        if 0 < m < G:
+            ds = [r for r in last if r >= G]
+            if ds:
+                yc = [(ds, mask_of(m, ds))]
+                for r in ds:
+                    ya_inc[r][m] = _bits(yc[0][1])
+        y_calls.append(yc)
+    return dict(unit=unit, last=last, seg_range=seg_range, off=off, width=width, rows_calls=rows_calls,
+                p_calls=p_calls, y_calls=y_calls, rw_inc=rw_inc, pa_inc=pa_inc, ya_inc=ya_inc)
 
 
+_NG = N - G
 SCRATCH = {
     "lsb": ("sbuf", [128, (N + 1) * TW], "bfloat16"),
     "seg": ("sbuf", [128, max(1, build_plan(CORES, comms_topo)["width"]) * TW], "bfloat16"),
     "pb": ("sbuf", [128, N * TW], "bfloat16"),
     "ysb": ("sbuf", [128, N * TW], "bfloat16"),
+    "zb": ("sbuf", [128, N * TW], "bfloat16"),
+    "at": ("sbuf", [128, max(1, _NG * (_NG - 1) // 2) * TW], "bfloat16"),
+    "one": ("sbuf", [128, TW], "bfloat16"),
+    "idn": ("sbuf", [128, TW], "bfloat16"),
     "c0": ("psum", [128, 512], "float32"),
     "c1": ("psum", [128, 512], "float32"),
     "a0": ("psum", [128, 512], "float32"),
     "a1": ("psum", [128, 512], "float32"),
+    "t0": ("psum", [128, 512], "float32"),
+    "t1": ("psum", [128, 512], "float32"),
 }
-SEMAPHORES = ["ldl", "ldb", "st", "sent"] + [p + str(i) for p in ("rw", "pa", "mm", "vy", "am", "vp") for i in range(N)]
+SEMAPHORES = ["ldl", "ldb", "st", "sent", "ms", "idr"] + [
+    p + str(i) for p in ("rw", "pa", "ya", "mm", "vy", "am", "vp", "tm", "tv", "zm", "zv") for i in range(N)]
 
 
 def rank_program(g, core, T, topo):
@@ -137,7 +140,8 @@ def rank_program(g, core, T, topo):
     cores = list(T.cores)
     n = len(cores)
     P = build_plan(cores, topo)
-    grp, g0, unit, seg_range, off = P["grp"], P["g0"], P["unit"], P["seg_range"], P["off"]
+    unit, seg_range, off = P["unit"], P["seg_range"], P["off"]
+    fed_y = r >= G and r in P["last"]
     queues = {"g": g, "t": g.tensor, "v": g.vector, "s": g.sync}
     waited = {"g": {}, "t": {}, "v": {}, "s": {}}
 
@@ -155,20 +159,31 @@ def rank_program(g, core, T, topo):
         return (cols(T.seg, off[r][m] + e - seg_range(r, m)[0]), "rw%d" % m, P["rw_inc"][r][m])
 
     def p_src(t):
-        if grp[t] == 0:
-            return ext(t, 0)
         if t in unit[r]:
             return (cols(T.pb, t), "vp%d" % t, 1)
         return (cols(T.pb, t), "pa%d" % unit[t][0], P["pa_inc"][r][unit[t][0]])
 
     def y_src(t):
-        if t == g0[t]:
-            return p_src(t)
+        if t == 0:
+            return ext(0, 0)
+        if fed_y:
+            return (cols(T.ysb, t), "ya%d" % t, P["ya_inc"][r][t])
         return (cols(T.ysb, t), "vy%d" % t, 1)
+
+    def z_src(s):
+        if s == r - 1:
+            return ext(r, 1 + s)
+        return (cols(T.zb, s), "zv%d" % s, 1)
 
     if r >= 1:
         g.sync.dma_start(T.lsb[:, TW:(r + 1) * TW], T.l[:, 0:r * TW]).then_inc(T.sem.ldl, 16)
     g.scalar.dma_start(T.lsb[:, 0:TW], T.b[:, :]).then_inc(T.sem.ldb, 16)
+
+    eliminate = r >= G + 2
+    if eliminate:
+        g.vector.memset(T.one[:, :], 1.0).then_inc(T.sem.ms, 1)
+        need("g", "ms", 1)
+        g.affine_select(T.idn[:, :], T.one[:, :], [[-1, TW]], AluOpType.is_equal, 0.0, 0, 1).then_inc(T.sem.idr, 1)
 
     sent = [0]
 
@@ -193,60 +208,127 @@ def rank_program(g, core, T, topo):
             need("g", "ldl", 16)
         send(cols(T.lsb, e0, e1 - e0), lambda d: cols(T.seg, off[d][r], e1 - e0), dests, mask, "rw%d" % r)
 
-    gr0 = g0[r]
-    has_dests = unit[r][-1] < n - 1
-    accrows = [m for m in unit[r] if m <= r or has_dests] if grp[r] >= 1 else []
-    accbank = [T.a0[:, 0:TW], T.a1[:, 0:TW]]
     chain = [T.c0[:, 0:TW], T.c1[:, 0:TW]]
-    last_user = [None, None]
-    ci = 0
-    for t in range(r + 1):
-        G = g0[t]
-        if t > G:
-            bank = chain[ci % 2]
-            if last_user[ci % 2] is not None:
-                need("t", "vy%d" % last_user[ci % 2], 1)
-            last_user[ci % 2] = t
-            ci += 1
+    accbank = [T.a0[:, 0:TW], T.a1[:, 0:TW]]
+    tbank = [T.t0, T.t1]
+    reader = {"c": [None, None], "t": [None, None]}
+    turn = {"c": 0, "t": 0}
+
+    def take(kind):
+        i = turn[kind] % 2
+        turn[kind] += 1
+        if reader[kind][i] is not None:
+            need("t", reader[kind][i], 1)
+        return i
+
+    def mm(out, lhs, rhs, start, stop):
+        need("t", lhs[1], lhs[2])
+        need("t", rhs[1], rhs[2])
+        return g.tensor.matmul(out, lhs[0], rhs[0], start, stop)
+
+    def minus(out, a, bank, mmsem, outsem):
+        need("v", mmsem, 1)
+        need("v", a[1], a[2])
+        g.vector.tensor_tensor(out, a[0], bank, AluOpType.subtract).then_inc(T.sem[outsem], 1)
+
+    def triangle_step(t):
+        i = take("c")
+        for s in range(t):
+            ins = mm(chain[i], ext(t, 1 + s), y_src(s), s == 0, s == t - 1)
+        ins.then_inc(T.sem["mm%d" % t], 1)
+        minus(cols(T.ysb, t), ext(t, 0), chain[i], "mm%d" % t, "vy%d" % t)
+        reader["c"][i] = "vy%d" % t
+
+    def at_slot(t, s):
+        k = t - G - 1
+        return k * (k + 1) // 2 + (s - G)
+
+    def eliminate_triangle():
+        for t in range(G + 1, r):
+            i = take("t")
+            w = t - G
             for s in range(G, t):
-                la, ls, lv = ext(t, 1 + s)
-                ya, ys, yv = y_src(s)
-                need("t", ls, lv)
-                need("t", ys, yv)
-                ins = g.tensor.matmul(bank, la, ya, s == G, s == t - 1)
-                if s == t - 1:
-                    ins.then_inc(T.sem["mm%d" % t], 1)
-            pa, ps, pv = p_src(t)
-            need("v", "mm%d" % t, 1)
-            need("v", ps, pv)
-            g.vector.tensor_tensor(cols(T.ysb, t), pa, bank, AluOpType.subtract).then_inc(T.sem["vy%d" % t], 1)
-        if 1 <= t <= gr0 and accrows:
-            s = t - 1
-            ya, ys, yv = y_src(s)
-            for i, m in enumerate(accrows):
-                la, ls, lv = ext(m, 1 + s)
-                need("t", ls, lv)
-                need("t", ys, yv)
-                ins = g.tensor.matmul(accbank[i], la, ya, s == 0, s == gr0 - 1)
-                if s == gr0 - 1:
+                mm(tbank[i][:, (s - G) * TW:(s - G + 1) * TW], ext(t, 1 + s), (T.idn[:, :], "idr", 1), True,
+                   True).then_inc(T.sem["tm%d" % t], 1)
+            need("v", "tm%d" % t, w)
+            g.vector.tensor_copy(cols(T.at, at_slot(t, G), w), tbank[i][:, 0:w * TW]).then_inc(T.sem["tv%d" % t], 1)
+            reader["t"][i] = "tv%d" % t
+        for s in range(r - 2, G - 1, -1):
+            i = take("c")
+            for t in range(r - 1, s, -1):
+                ins = mm(chain[i], (cols(T.at, at_slot(t, s)), "tv%d" % t, 1), z_src(t), t == r - 1, t == s + 1)
+            ins.then_inc(T.sem["zm%d" % s], 1)
+            minus(cols(T.zb, s), ext(r, 1 + s), chain[i], "zm%d" % s, "zv%d" % s)
+            reader["c"][i] = "zv%d" % s
+
+    if r < G:
+        for t in range(1, r + 1):
+            triangle_step(t)
+        y_own = y_src(r)
+    elif not fed_y:
+        rows = list(unit[r])
+        others = [m for m in rows if m != r]
+
+        def acc(m, s):
+            ins = mm(accbank[rows.index(m)], ext(m, 1 + s), y_src(s), s == 0, s == G - 1)
+            if s == G - 1:
+                ins.then_inc(T.sem["am%d" % m], 1)
+
+        for t in range(1, G + 1):
+            if t == G - 1:
+                for m in others:
+                    for s in range(G - 2):
+                        acc(m, s)
+            if t < G:
+                triangle_step(t)
+            acc(r, t - 1)
+            if t >= G - 1:
+                for m in others:
+                    acc(m, t - 1)
+        for m in rows:
+            minus(cols(T.pb, m), ext(m, 0), accbank[rows.index(m)], "am%d" % m, "vp%d" % m)
+        if eliminate:
+            eliminate_triangle()
+        if r > G:
+            i = take("c")
+            ss = [s for s in range(r - 1, G - 1, -1) if s in unit[r]] + \
+                 [s for s in range(r - 1, G - 1, -1) if s not in unit[r]]
+            for k, s in enumerate(ss):
+                ins = mm(chain[i], z_src(s), p_src(s), k == 0, k == len(ss) - 1)
+            ins.then_inc(T.sem["mm%d" % r], 1)
+            minus(cols(T.ysb, r), p_src(r), chain[i], "mm%d" % r, "vy%d" % r)
+            y_own = (cols(T.ysb, r), "vy%d" % r, 1)
+        else:
+            y_own = p_src(r)
+    else:
+        rows = [m for m in unit[r] if m <= r]
+        if eliminate:
+            eliminate_triangle()
+        for s in range(G):
+            for m in rows:
+                ins = mm(accbank[rows.index(m)], ext(m, 1 + s), y_src(s), s == 0, m != r and s == G - 1)
+                if m != r and s == G - 1:
                     ins.then_inc(T.sem["am%d" % m], 1)
-            if t == gr0:
-                for i, m in enumerate(accrows):
-                    ba, bs, bv = ext(m, 0)
-                    need("v", "am%d" % m, 1)
-                    need("v", bs, bv)
-                    g.vector.tensor_tensor(cols(T.pb, m), ba, accbank[i], AluOpType.subtract).then_inc(
-                        T.sem["vp%d" % m], 1)
+        for m in rows:
+            if m != r:
+                minus(cols(T.pb, m), ext(m, 0), accbank[rows.index(m)], "am%d" % m, "vp%d" % m)
+        for s in range(G, r):
+            ins = mm(accbank[rows.index(r)], z_src(s), p_src(s), False, s == r - 1)
+        ins.then_inc(T.sem["mm%d" % r], 1)
+        minus(cols(T.ysb, r), ext(r, 0), accbank[rows.index(r)], "mm%d" % r, "vy%d" % r)
+        y_own = (cols(T.ysb, r), "vy%d" % r, 1)
 
     u = unit[r]
     for dests, mask in P["p_calls"][r]:
         for m in u:
             need("g", "vp%d" % m, 1)
         send(cols(T.pb, u[0], len(u)), lambda d: cols(T.pb, u[0], len(u)), dests, mask, "pa%d" % u[0])
+    for dests, mask in P["y_calls"][r]:
+        need("g", y_own[1], y_own[2])
+        send(y_own[0], lambda d: cols(T.ysb, r), dests, mask, "ya%d" % r)
     if sent[0]:
         g.wait_ge(T.sem.sent, sent[0])
 
-    ya, ys, yv = y_src(r)
-    need("s", ys, yv)
-    g.sync.dma_start(T.y[:, :], ya).then_inc(T.sem.st, 16)
+    need("s", y_own[1], y_own[2])
+    g.sync.dma_start(T.y[:, :], y_own[0]).then_inc(T.sem.st, 16)
     g.sync.wait_ge(T.sem.st, 16)

@@ -32,10 +32,16 @@ def build_plan(cores, topo):
             t += 1
         t += 1
     last = unit[n - 1]
+    yunit = [None] * n
+    for t in range(n):
+        mem = tuple(q for q in range(n) if duo[q] == duo[t] and q < G)
+        yunit[t] = mem if (t < G and duo[t] > 0 and len(mem) == 2) else (t,)
 
     def seg_range(r, m):
         if m == r:
             return None
+        if r < G:
+            return (0, m + 1) if (m < r or m in yunit[r]) else None
         if m in unit[r]:
             if m < r:
                 return (0, m + 1)
@@ -43,7 +49,7 @@ def build_plan(cores, topo):
         if m > r:
             return None
         if m < G:
-            return None if (r in last and m > 0) else (0, m + 1)
+            return (0, 1) if m == 0 else None
         return (G + 1, m + 1) if m > G else None
 
     off, width = [], 0
@@ -70,15 +76,17 @@ def build_plan(cores, topo):
     for m in range(n):
         dests = [r for r in range(n) if seg_range(r, m)]
         if m < G:
-            order = ([r for r in dests if r >= G and r not in last] + [r for r in dests if r < G]
-                     + [r for r in dests if r in last])
+            order = (sorted([r for r in dests if r < G and r not in yunit[m]], key=lambda r: (-duo[r], r))
+                     + [r for r in dests if r < G and r in yunit[m]]
+                     + [r for r in dests if r >= G and r not in last] + [r for r in dests if r in last])
         else:
             order = (sorted([r for r in dests if r not in unit[m]], key=lambda r: (-duo[r], r))
                      + [r for r in dests if r in unit[m]])
         calls = []
         for r in order:
             rg = seg_range(r, m)
-            if calls and calls[-1][0] == rg and duo[calls[-1][1][-1]] == duo[r]:
+            prev = calls[-1][1][-1] if calls else None
+            if calls and calls[-1][0] == rg and (duo[prev] == duo[r] if m >= G else (prev < G) == (r < G)):
                 calls[-1][1].append(r)
             else:
                 calls.append((rg, [r]))
@@ -102,13 +110,18 @@ def build_plan(cores, topo):
         p_calls.append(pc)
         yc = []
         if 0 < m < G:
-            ds = [r for r in last if r >= G]
+            yu = yunit[m]
+            ds = []
+            for r in [q for q in range(G, n) if q not in last] + [q for q in last if q >= G]:
+                srv = [q for q in yu if topo.same_plane(cores[q], cores[r])]
+                if (srv[0] if srv else yu[0]) == m:
+                    ds.append(r)
             if ds:
                 yc = [(ds, mask_of(m, ds))]
                 for r in ds:
-                    ya_inc[r][m] = _bits(yc[0][1])
+                    ya_inc[r][yu[0]] = _bits(yc[0][1])
         y_calls.append(yc)
-    return dict(unit=unit, last=last, seg_range=seg_range, off=off, width=width, rows_calls=rows_calls,
+    return dict(unit=unit, yunit=yunit, last=last, seg_range=seg_range, off=off, width=width, rows_calls=rows_calls,
                 p_calls=p_calls, y_calls=y_calls, rw_inc=rw_inc, pa_inc=pa_inc, ya_inc=ya_inc)
 
 
@@ -141,7 +154,8 @@ def rank_program(g, core, T, topo):
     n = len(cores)
     P = build_plan(cores, topo)
     unit, seg_range, off = P["unit"], P["seg_range"], P["off"]
-    fed_y = r >= G and r in P["last"]
+    fed_y = r >= G
+    is_last = r >= G and r in P["last"]
     queues = {"g": g, "t": g.tensor, "v": g.vector, "s": g.sync}
     waited = {"g": {}, "t": {}, "v": {}, "s": {}}
 
@@ -167,7 +181,8 @@ def rank_program(g, core, T, topo):
         if t == 0:
             return ext(0, 0)
         if fed_y:
-            return (cols(T.ysb, t), "ya%d" % t, P["ya_inc"][r][t])
+            lead = P["yunit"][t][0]
+            return (cols(T.ysb, t), "ya%d" % lead, P["ya_inc"][r][lead])
         return (cols(T.ysb, t), "vy%d" % t, 1)
 
     def z_src(s):
@@ -262,29 +277,20 @@ def rank_program(g, core, T, topo):
             reader["c"][i] = "zv%d" % s
 
     if r < G:
-        for t in range(1, r + 1):
+        for t in range(1, P["yunit"][r][-1] + 1):
             triangle_step(t)
         y_own = y_src(r)
-    elif not fed_y:
+    elif not is_last:
         rows = list(unit[r])
-        others = [m for m in rows if m != r]
 
         def acc(m, s):
             ins = mm(accbank[rows.index(m)], ext(m, 1 + s), y_src(s), s == 0, s == G - 1)
             if s == G - 1:
                 ins.then_inc(T.sem["am%d" % m], 1)
 
-        for t in range(1, G + 1):
-            if t == G - 1:
-                for m in others:
-                    for s in range(G - 2):
-                        acc(m, s)
-            if t < G:
-                triangle_step(t)
-            acc(r, t - 1)
-            if t >= G - 1:
-                for m in others:
-                    acc(m, t - 1)
+        for s in range(G):
+            for m in rows:
+                acc(m, s)
         for m in rows:
             minus(cols(T.pb, m), ext(m, 0), accbank[rows.index(m)], "am%d" % m, "vp%d" % m)
         if eliminate:
@@ -324,8 +330,10 @@ def rank_program(g, core, T, topo):
             need("g", "vp%d" % m, 1)
         send(cols(T.pb, u[0], len(u)), lambda d: cols(T.pb, u[0], len(u)), dests, mask, "pa%d" % u[0])
     for dests, mask in P["y_calls"][r]:
-        need("g", y_own[1], y_own[2])
-        send(y_own[0], lambda d: cols(T.ysb, r), dests, mask, "ya%d" % r)
+        yu = P["yunit"][r]
+        for m in yu:
+            need("g", "vy%d" % m, 1)
+        send(cols(T.ysb, yu[0], len(yu)), lambda d: cols(T.ysb, yu[0], len(yu)), dests, mask, "ya%d" % yu[0])
     if sent[0]:
         g.wait_ge(T.sem.sent, sent[0])
 

@@ -5,7 +5,7 @@ from concourse.mybir import AluOpType
 CORES = [211, 219, 227, 235, 243, 251, 83, 91, 99, 107, 115, 123]
 N = 12
 TW = 128
-G = 6
+G = 4
 
 
 def _bits(m):
@@ -37,20 +37,16 @@ def build_plan(cores, topo):
         mem = tuple(q for q in range(n) if duo[q] == duo[t] and q < G)
         yunit[t] = mem if (t < G and duo[t] > 0 and len(mem) == 2) else (t,)
 
+    nb = [(r - 1 - G) // 2 if (r >= G + 2 and r not in last) else 0 for r in range(n)]
+
     def seg_range(r, m):
         if m == r:
             return None
         if r < G:
             return (0, m + 1) if (m < r or m in yunit[r]) else None
         if m in unit[r]:
-            if m < r:
-                return (0, m + 1)
-            return (0, G + 1) if r not in last else None
-        if m > r:
-            return None
-        if m < G:
-            return (0, 1) if m == 0 else None
-        return (G + 1, m + 1) if m > G else None
+            return (0, G + 1) if (m < r or r not in last) else None
+        return (0, 1) if m == 0 else None
 
     off, width = [], 0
     for r in range(n):
@@ -69,7 +65,8 @@ def build_plan(cores, topo):
             k &= topo.mask(cores[src], cores[d])
         return k
 
-    rows_calls, p_calls, y_calls = [], [], []
+    rows_calls, p_calls, y_calls, at_calls = [], [], [], []
+    at_inc = [dict() for _ in range(n)]
     rw_inc = [dict() for _ in range(n)]
     pa_inc = [dict() for _ in range(n)]
     ya_inc = [dict() for _ in range(n)]
@@ -80,13 +77,12 @@ def build_plan(cores, topo):
                      + [r for r in dests if r < G and r in yunit[m]]
                      + [r for r in dests if r >= G and r not in last] + [r for r in dests if r in last])
         else:
-            order = (sorted([r for r in dests if r not in unit[m]], key=lambda r: (-duo[r], r))
-                     + [r for r in dests if r in unit[m]])
+            order = dests
         calls = []
         for r in order:
             rg = seg_range(r, m)
             prev = calls[-1][1][-1] if calls else None
-            if calls and calls[-1][0] == rg and (duo[prev] == duo[r] if m >= G else (prev < G) == (r < G)):
+            if calls and calls[-1][0] == rg and (prev < G) == (r < G):
                 calls[-1][1].append(r)
             else:
                 calls.append((rg, [r]))
@@ -95,6 +91,17 @@ def build_plan(cores, topo):
             for r in ds:
                 rw_inc[r][m] = _bits(k)
         rows_calls.append(calls)
+        ac = []
+        if G < m < n - 1:
+            later = sorted(range(m + 1, n), key=lambda r: (-duo[r], not topo.same_plane(cores[m], cores[r])))
+            early = [r for r in later if m >= r - nb[r]]
+            for ds in (early + [r for r in later if r in last],
+                       [r for r in later if r not in last and r not in early]):
+                if ds:
+                    ac.append((ds, mask_of(m, ds)))
+                    for r in ds:
+                        at_inc[r][m] = _bits(ac[-1][1])
+        at_calls.append(ac)
         pc = []
         if m >= G:
             u = unit[m]
@@ -122,7 +129,8 @@ def build_plan(cores, topo):
                     ya_inc[r][yu[0]] = _bits(yc[0][1])
         y_calls.append(yc)
     return dict(unit=unit, yunit=yunit, last=last, seg_range=seg_range, off=off, width=width, rows_calls=rows_calls,
-                p_calls=p_calls, y_calls=y_calls, rw_inc=rw_inc, pa_inc=pa_inc, ya_inc=ya_inc)
+                p_calls=p_calls, y_calls=y_calls, at_calls=at_calls, at_inc=at_inc, rw_inc=rw_inc, pa_inc=pa_inc,
+                ya_inc=ya_inc, nb=nb)
 
 
 _NG = N - G
@@ -139,10 +147,9 @@ SCRATCH = {
     "c1": ("psum", [128, 512], "float32"),
     "a0": ("psum", [128, 512], "float32"),
     "a1": ("psum", [128, 512], "float32"),
-    "t0": ("psum", [128, 512], "float32"),
-    "t1": ("psum", [128, 512], "float32"),
+    "t0": ("psum", [128, 1024], "bfloat16"),
 }
-SEMAPHORES = ["ldl", "ldb", "st", "sent", "ms", "idr"] + [
+SEMAPHORES = ["ldl", "ldb", "ldf", "st", "sent", "ms", "idr"] + [
     p + str(i) for p in ("rw", "pa", "ya", "mm", "vy", "am", "vp", "tm", "tv", "zm", "zv") for i in range(N)]
 
 
@@ -169,7 +176,7 @@ def rank_program(g, core, T, topo):
 
     def ext(m, e):
         if m == r:
-            return (cols(T.lsb, e), "ldb" if e == 0 else "ldl", 16)
+            return (cols(T.lsb, e), "ldb" if e == 0 else ("ldf" if (r >= G and e <= G) else "ldl"), 16)
         return (cols(T.seg, off[r][m] + e - seg_range(r, m)[0]), "rw%d" % m, P["rw_inc"][r][m])
 
     def p_src(t):
@@ -190,12 +197,18 @@ def rank_program(g, core, T, topo):
             return ext(r, 1 + s)
         return (cols(T.zb, s), "zv%d" % s, 1)
 
-    if r >= 1:
-        g.sync.dma_start(T.lsb[:, TW:(r + 1) * TW], T.l[:, 0:r * TW]).then_inc(T.sem.ldl, 16)
-    g.scalar.dma_start(T.lsb[:, 0:TW], T.b[:, :]).then_inc(T.sem.ldb, 16)
+    if r < G:
+        if r >= 1:
+            g.sync.dma_start(T.lsb[:, TW:(r + 1) * TW], T.l[:, 0:r * TW]).then_inc(T.sem.ldl, 16)
+        g.scalar.dma_start(T.lsb[:, 0:TW], T.b[:, :]).then_inc(T.sem.ldb, 16)
+    else:
+        if r > G:
+            g.sync.dma_start(T.lsb[:, (G + 1) * TW:(r + 1) * TW], T.l[:, G * TW:r * TW]).then_inc(T.sem.ldl, 16)
+        g.scalar.dma_start(T.lsb[:, TW:(G + 1) * TW], T.l[:, 0:G * TW]).then_inc(T.sem.ldf, 16)
+        g.sync.dma_start(T.lsb[:, 0:TW], T.b[:, :]).then_inc(T.sem.ldb, 16)
 
-    eliminate = r >= G + 2
-    if eliminate:
+    zsteps = list(range(r - 2, G - 1, -1)) if r >= G + 2 else []
+    if P["at_calls"][r]:
         g.vector.memset(T.one[:, :], 1.0).then_inc(T.sem.ms, 1)
         need("g", "ms", 1)
         g.affine_select(T.idn[:, :], T.one[:, :], [[-1, TW]], AluOpType.is_equal, 0.0, 0, 1).then_inc(T.sem.idr, 1)
@@ -220,14 +233,13 @@ def rank_program(g, core, T, topo):
         if e0 == 0:
             need("g", "ldb", 16)
         if e1 > 1:
-            need("g", "ldl", 16)
+            need("g", "ldf" if r >= G else "ldl", 16)
         send(cols(T.lsb, e0, e1 - e0), lambda d: cols(T.seg, off[d][r], e1 - e0), dests, mask, "rw%d" % r)
 
     chain = [T.c0[:, 0:TW], T.c1[:, 0:TW]]
     accbank = [T.a0[:, 0:TW], T.a1[:, 0:TW]]
-    tbank = [T.t0, T.t1]
-    reader = {"c": [None, None], "t": [None, None]}
-    turn = {"c": 0, "t": 0}
+    reader = {"c": [None, None]}
+    turn = {"c": 0}
 
     def take(kind):
         i = turn[kind] % 2
@@ -258,23 +270,28 @@ def rank_program(g, core, T, topo):
         k = t - G - 1
         return k * (k + 1) // 2 + (s - G)
 
-    def eliminate_triangle():
-        for t in range(G + 1, r):
-            i = take("t")
-            w = t - G
-            for s in range(G, t):
-                mm(tbank[i][:, (s - G) * TW:(s - G + 1) * TW], ext(t, 1 + s), (T.idn[:, :], "idr", 1), True,
-                   True).then_inc(T.sem["tm%d" % t], 1)
-            need("v", "tm%d" % t, w)
-            g.vector.tensor_copy(cols(T.at, at_slot(t, G), w), tbank[i][:, 0:w * TW]).then_inc(T.sem["tv%d" % t], 1)
-            reader["t"][i] = "tv%d" % t
-        for s in range(r - 2, G - 1, -1):
+    def eliminate_triangle(steps):
+        for s in steps:
             i = take("c")
             for t in range(r - 1, s, -1):
-                ins = mm(chain[i], (cols(T.at, at_slot(t, s)), "tv%d" % t, 1), z_src(t), t == r - 1, t == s + 1)
+                ins = mm(chain[i], (cols(T.at, at_slot(t, s)), "tv%d" % t, P["at_inc"][r][t]), z_src(t), t == r - 1,
+                         t == s + 1)
             ins.then_inc(T.sem["zm%d" % s], 1)
             minus(cols(T.zb, s), ext(r, 1 + s), chain[i], "zm%d" % s, "zv%d" % s)
             reader["c"][i] = "zv%d" % s
+
+    if P["at_calls"][r]:
+        w = r - G
+        need("t", "ldl", 16)
+        need("t", "idr", 1)
+        for s in range(G, r):
+            g.tensor.transpose(T.t0[:, (s - G) * TW:(s - G + 1) * TW], cols(T.lsb, 1 + s),
+                               T.idn[:, :]).then_inc(T.sem["tm%d" % r], 1)
+        need("v", "tm%d" % r, w)
+        g.vector.tensor_copy(cols(T.at, at_slot(r, G), w), T.t0[:, 0:w * TW]).then_inc(T.sem["tv%d" % r], 1)
+        need("g", "tv%d" % r, 1)
+        for dests, mask in P["at_calls"][r]:
+            send(cols(T.at, at_slot(r, G), w), lambda d: cols(T.at, at_slot(r, G), w), dests, mask, "tv%d" % r)
 
     if r < G:
         for t in range(1, P["yunit"][r][-1] + 1):
@@ -288,13 +305,13 @@ def rank_program(g, core, T, topo):
             if s == G - 1:
                 ins.then_inc(T.sem["am%d" % m], 1)
 
+        eliminate_triangle(zsteps[:P["nb"][r]])
         for s in range(G):
             for m in rows:
                 acc(m, s)
         for m in rows:
             minus(cols(T.pb, m), ext(m, 0), accbank[rows.index(m)], "am%d" % m, "vp%d" % m)
-        if eliminate:
-            eliminate_triangle()
+        eliminate_triangle(zsteps[P["nb"][r]:])
         if r > G:
             i = take("c")
             ss = [s for s in range(r - 1, G - 1, -1) if s in unit[r]] + \
@@ -308,8 +325,7 @@ def rank_program(g, core, T, topo):
             y_own = p_src(r)
     else:
         rows = [m for m in unit[r] if m <= r]
-        if eliminate:
-            eliminate_triangle()
+        eliminate_triangle(zsteps)
         for s in range(G):
             for m in rows:
                 ins = mm(accbank[rows.index(m)], ext(m, 1 + s), y_src(s), s == 0, m != r and s == G - 1)
@@ -318,8 +334,9 @@ def rank_program(g, core, T, topo):
         for m in rows:
             if m != r:
                 minus(cols(T.pb, m), ext(m, 0), accbank[rows.index(m)], "am%d" % m, "vp%d" % m)
-        for s in range(G, r):
-            ins = mm(accbank[rows.index(r)], z_src(s), p_src(s), False, s == r - 1)
+        ss = [s for s in range(G, r) if s in unit[r]] + [s for s in range(G, r) if s not in unit[r]]
+        for k, s in enumerate(ss):
+            ins = mm(accbank[rows.index(r)], z_src(s), p_src(s), False, k == len(ss) - 1)
         ins.then_inc(T.sem["mm%d" % r], 1)
         minus(cols(T.ysb, r), ext(r, 0), accbank[rows.index(r)], "mm%d" % r, "vy%d" % r)
         y_own = (cols(T.ysb, r), "vy%d" % r, 1)

import comms_topo
from concourse.bass import DstId, RemoteDMATransfer
from concourse.mybir import AluOpType

CORES = [211, 219, 227, 235, 243, 251, 83, 91, 99, 107, 115, 123]
N = 12
TW = 128
G = 4


def _bits(m):
    n = 0
    while m:
        n += m & 1
        m >>= 1
    return n


def build_plan(cores, topo):
    n = len(cores)
    unit, duo = [None] * n, [None] * n
    t = 0
    while t < n:
        pair = t + 1 < n and (t < G) == (t + 1 < G) and topo.mates(cores[t], cores[t + 1])
        duo[t] = t
        unit[t] = (t,)
        if pair:
            duo[t + 1] = t
            unit[t + 1] = (t + 1,)
            if t >= G:
                unit[t] = unit[t + 1] = (t, t + 1)
            t += 1
        t += 1
    last = unit[n - 1]
    yunit = [None] * n
    for t in range(n):
        mem = tuple(q for q in range(n) if duo[q] == duo[t] and q < G)
        yunit[t] = mem if (t < G and duo[t] > 0 and len(mem) == 2) else (t,)

    nb = [(r - 1 - G) // 2 if (r >= G + 2 and r not in last) else 0 for r in range(n)]

    def seg_range(r, m):
        if m == r:
            return None
        if r < G:
            return (0, m + 1) if (m < r or m in yunit[r]) else None
        if m in unit[r]:
            return (0, G + 1) if (m < r or r not in last) else None
        return (0, 1) if m == 0 else None

    off, width = [], 0
    for r in range(n):
        o, d = 0, {}
        for m in range(n):
            rg = seg_range(r, m)
            if rg:
                d[m] = o
                o += rg[1] - rg[0]
        off.append(d)
        width = max(width, o)

    def mask_of(src, dests):
        k = topo.mask(cores[src], cores[dests[0]])
        for d in dests[1:]:
            k &= topo.mask(cores[src], cores[d])
        return k

    rows_calls, p_calls, y_calls, at_calls = [], [], [], []
    at_inc = [dict() for _ in range(n)]
    rw_inc = [dict() for _ in range(n)]
    pa_inc = [dict() for _ in range(n)]
    ya_inc = [dict() for _ in range(n)]
    for m in range(n):
        dests = [r for r in range(n) if seg_range(r, m)]
        if m < G:
            order = (sorted([r for r in dests if r < G and r not in yunit[m]], key=lambda r: (-duo[r], r))
                     + [r for r in dests if r < G and r in yunit[m]]
                     + [r for r in dests if r >= G and r not in last] + [r for r in dests if r in last])
        else:
            order = dests
        calls = []
        for r in order:
            rg = seg_range(r, m)
            prev = calls[-1][1][-1] if calls else None
            if calls and calls[-1][0] == rg and (prev < G) == (r < G):
                calls[-1][1].append(r)
            else:
                calls.append((rg, [r]))
        calls = [(rg, ds, mask_of(m, ds)) for rg, ds in calls]
        for rg, ds, k in calls:
            for r in ds:
                rw_inc[r][m] = _bits(k)
        rows_calls.append(calls)
        ac = []
        if G < m < n - 1:
            later = sorted(range(m + 1, n), key=lambda r: (-duo[r], not topo.same_plane(cores[m], cores[r])))
            early = [r for r in later if m >= r - nb[r]]
            for ds in (early + [r for r in later if r in last],
                       [r for r in later if r not in last and r not in early]):
                if ds:
                    ac.append((ds, mask_of(m, ds)))
                    for r in ds:
                        at_inc[r][m] = _bits(ac[-1][1])
        at_calls.append(ac)
        pc = []
        if m >= G:
            u = unit[m]
            mine = []
            for r in range(n - 1, u[-1], -1):
                srv = [q for q in u if topo.same_plane(cores[q], cores[r])]
                if (srv[0] if srv else u[0]) == m:
                    mine.append(r)
            if mine:
                pc = [(mine, mask_of(m, mine))]
                for r in mine:
                    pa_inc[r][u[0]] = _bits(pc[0][1])
        p_calls.append(pc)
        yc = []
        if 0 < m < G:
            yu = yunit[m]
            ds = []
            for r in [q for q in range(G, n) if q not in last] + [q for q in last if q >= G]:
                srv = [q for q in yu if topo.same_plane(cores[q], cores[r])]
                if (srv[0] if srv else yu[0]) == m:
                    ds.append(r)
            if ds:
                yc = [(ds, mask_of(m, ds))]
                for r in ds:
                    ya_inc[r][yu[0]] = _bits(yc[0][1])
        y_calls.append(yc)
    return dict(unit=unit, yunit=yunit, last=last, seg_range=seg_range, off=off, width=width, rows_calls=rows_calls,
                p_calls=p_calls, y_calls=y_calls, at_calls=at_calls, at_inc=at_inc, rw_inc=rw_inc, pa_inc=pa_inc,
                ya_inc=ya_inc, nb=nb)


_NG = N - G
SCRATCH = {
    "lsb": ("sbuf", [128, (N + 1) * TW], "bfloat16"),
    "seg": ("sbuf", [128, max(1, build_plan(CORES, comms_topo)["width"]) * TW], "bfloat16"),
    "pb": ("sbuf", [128, N * TW], "bfloat16"),
    "ysb": ("sbuf", [128, N * TW], "bfloat16"),
    "zb": ("sbuf", [128, N * TW], "bfloat16"),
    "at": ("sbuf", [128, max(1, _NG * (_NG - 1) // 2) * TW], "bfloat16"),
    "one": ("sbuf", [128, TW], "bfloat16"),
    "idn": ("sbuf", [128, TW], "bfloat16"),
    "c0": ("psum", [128, 512], "float32"),
    "c1": ("psum", [128, 512], "float32"),
    "a0": ("psum", [128, 512], "float32"),
    "a1": ("psum", [128, 512], "float32"),
    "t0": ("psum", [128, 1024], "bfloat16"),
}
SEMAPHORES = ["ldl", "ldb", "ldf", "st", "sent", "ms", "idr"] + [
    p + str(i) for p in ("rw", "pa", "ya", "mm", "vy", "am", "vp", "tm", "tv", "zm", "zv") for i in range(N)]


def rank_program(g, core, T, topo):
    r = T.rank_of(core)
    if r is None:
        return
    cores = list(T.cores)
    n = len(cores)
    P = build_plan(cores, topo)
    unit, seg_range, off = P["unit"], P["seg_range"], P["off"]
    fed_y = r >= G
    is_last = r >= G and r in P["last"]
    queues = {"g": g, "t": g.tensor, "v": g.vector, "s": g.sync}
    waited = {"g": {}, "t": {}, "v": {}, "s": {}}

    def need(q, sem, val):
        if waited[q].get(sem, 0) < val:
            queues[q].wait_ge(T.sem[sem], val)
            waited[q][sem] = val

    def cols(buf, k, w=1):
        return buf[:, k * TW:(k + w) * TW]

    def ext(m, e):
        if m == r:
            return (cols(T.lsb, e), "ldb" if e == 0 else ("ldf" if (r >= G and e <= G) else "ldl"), 16)
        return (cols(T.seg, off[r][m] + e - seg_range(r, m)[0]), "rw%d" % m, P["rw_inc"][r][m])

    def p_src(t):
        if t in unit[r]:
            return (cols(T.pb, t), "vp%d" % t, 1)
        return (cols(T.pb, t), "pa%d" % unit[t][0], P["pa_inc"][r][unit[t][0]])

    def y_src(t):
        if t == 0:
            return ext(0, 0)
        if fed_y:
            lead = P["yunit"][t][0]
            return (cols(T.ysb, t), "ya%d" % lead, P["ya_inc"][r][lead])
        return (cols(T.ysb, t), "vy%d" % t, 1)

    def z_src(s):
        if s == r - 1:
            return ext(r, 1 + s)
        return (cols(T.zb, s), "zv%d" % s, 1)

    if r < G:
        if r >= 1:
            g.sync.dma_start(T.lsb[:, TW:(r + 1) * TW], T.l[:, 0:r * TW]).then_inc(T.sem.ldl, 16)
        g.scalar.dma_start(T.lsb[:, 0:TW], T.b[:, :]).then_inc(T.sem.ldb, 16)
    else:
        if r > G:
            g.sync.dma_start(T.lsb[:, (G + 1) * TW:(r + 1) * TW], T.l[:, G * TW:r * TW]).then_inc(T.sem.ldl, 16)
        g.scalar.dma_start(T.lsb[:, TW:(G + 1) * TW], T.l[:, 0:G * TW]).then_inc(T.sem.ldf, 16)
        g.sync.dma_start(T.lsb[:, 0:TW], T.b[:, :]).then_inc(T.sem.ldb, 16)

    zsteps = list(range(r - 2, G - 1, -1)) if r >= G + 2 else []
    if P["at_calls"][r]:
        g.vector.memset(T.one[:, :], 1.0).then_inc(T.sem.ms, 1)
        need("g", "ms", 1)
        g.affine_select(T.idn[:, :], T.one[:, :], [[-1, TW]], AluOpType.is_equal, 0.0, 0, 1).then_inc(T.sem.idr, 1)

    sent = [0]

    def send(src, dst_of, dests, mask, sem):
        if len(dests) == 1:
            rid, pid = topo.addr(cores[dests[0]], core)
            g.remote_dma(dst_of(dests[0]), src, T.sem[sem], T.sem.sent, pid, rid, mask)
        else:
            ids = []
            for d in dests:
                rid, pid = topo.addr(cores[d], core)
                ids.append(DstId(rid=rid, pnc=pid))
            g.remote_dma_fused([RemoteDMATransfer(dst_ids=ids, dma_engine_mask=mask, remote_sem=T.sem[sem],
                                                  srcs=[src], dsts=[dst_of(d) for d in dests], alu_op=0)],
                               local_sem=T.sem.sent)
        sent[0] += _bits(mask)

    for (e0, e1), dests, mask in P["rows_calls"][r]:
        if e0 == 0:
            need("g", "ldb", 16)
        if e1 > 1:
            need("g", "ldf" if r >= G else "ldl", 16)
        send(cols(T.lsb, e0, e1 - e0), lambda d: cols(T.seg, off[d][r], e1 - e0), dests, mask, "rw%d" % r)

    chain = [T.c0[:, 0:TW], T.c1[:, 0:TW]]
    accbank = [T.a0[:, 0:TW], T.a1[:, 0:TW]]
    reader = {"c": [None, None]}
    turn = {"c": 0}

    def take(kind):
        i = turn[kind] % 2
        turn[kind] += 1
        if reader[kind][i] is not None:
            need("t", reader[kind][i], 1)
        return i

    def mm(out, lhs, rhs, start, stop):
        need("t", lhs[1], lhs[2])
        need("t", rhs[1], rhs[2])
        return g.tensor.matmul(out, lhs[0], rhs[0], start, stop)

    def minus(out, a, bank, mmsem, outsem):
        need("v", mmsem, 1)
        need("v", a[1], a[2])
        g.vector.tensor_tensor(out, a[0], bank, AluOpType.subtract).then_inc(T.sem[outsem], 1)

    def triangle_step(t):
        i = take("c")
        for s in range(t):
            ins = mm(chain[i], ext(t, 1 + s), y_src(s), s == 0, s == t - 1)
        ins.then_inc(T.sem["mm%d" % t], 1)
        minus(cols(T.ysb, t), ext(t, 0), chain[i], "mm%d" % t, "vy%d" % t)
        reader["c"][i] = "vy%d" % t

    def at_slot(t, s):
        k = t - G - 1
        return k * (k + 1) // 2 + (s - G)

    def eliminate_triangle(steps):
        for s in steps:
            i = take("c")
            for t in range(r - 1, s, -1):
                ins = mm(chain[i], (cols(T.at, at_slot(t, s)), "tv%d" % t, P["at_inc"][r][t]), z_src(t), t == r - 1,
                         t == s + 1)
            ins.then_inc(T.sem["zm%d" % s], 1)
            minus(cols(T.zb, s), ext(r, 1 + s), chain[i], "zm%d" % s, "zv%d" % s)
            reader["c"][i] = "zv%d" % s

    if P["at_calls"][r]:
        w = r - G
        need("t", "ldl", 16)
        need("t", "idr", 1)
        for s in range(G, r):
            g.tensor.transpose(T.t0[:, (s - G) * TW:(s - G + 1) * TW], cols(T.lsb, 1 + s),
                               T.idn[:, :]).then_inc(T.sem["tm%d" % r], 1)
        need("v", "tm%d" % r, w)
        g.vector.tensor_copy(cols(T.at, at_slot(r, G), w), T.t0[:, 0:w * TW]).then_inc(T.sem["tv%d" % r], 1)
        need("g", "tv%d" % r, 1)
        for dests, mask in P["at_calls"][r]:
            send(cols(T.at, at_slot(r, G), w), lambda d: cols(T.at, at_slot(r, G), w), dests, mask, "tv%d" % r)

    if r < G:
        for t in range(1, P["yunit"][r][-1] + 1):
            triangle_step(t)
        y_own = y_src(r)
    elif not is_last:
        rows = list(unit[r])

        def acc(m, s):
            ins = mm(accbank[rows.index(m)], ext(m, 1 + s), y_src(s), s == 0, s == G - 1)
            if s == G - 1:
                ins.then_inc(T.sem["am%d" % m], 1)

        eliminate_triangle(zsteps[:P["nb"][r]])
        for s in range(G):
            for m in rows:
                acc(m, s)
        for m in rows:
            minus(cols(T.pb, m), ext(m, 0), accbank[rows.index(m)], "am%d" % m, "vp%d" % m)
        eliminate_triangle(zsteps[P["nb"][r]:])
        if r > G:
            i = take("c")
            ss = [s for s in range(r - 1, G - 1, -1) if s in unit[r]] + \
                 [s for s in range(r - 1, G - 1, -1) if s not in unit[r]]
            for k, s in enumerate(ss):
                ins = mm(chain[i], z_src(s), p_src(s), k == 0, k == len(ss) - 1)
            ins.then_inc(T.sem["mm%d" % r], 1)
            minus(cols(T.ysb, r), p_src(r), chain[i], "mm%d" % r, "vy%d" % r)
            y_own = (cols(T.ysb, r), "vy%d" % r, 1)
        else:
            y_own = p_src(r)
    else:
        rows = [m for m in unit[r] if m <= r]
        eliminate_triangle(zsteps)
        for s in range(G):
            for m in rows:
                ins = mm(accbank[rows.index(m)], ext(m, 1 + s), y_src(s), s == 0, m != r and s == G - 1)
                if m != r and s == G - 1:
                    ins.then_inc(T.sem["am%d" % m], 1)
        for m in rows:
            if m != r:
                minus(cols(T.pb, m), ext(m, 0), accbank[rows.index(m)], "am%d" % m, "vp%d" % m)
        ss = [s for s in range(G, r) if s in unit[r]] + [s for s in range(G, r) if s not in unit[r]]
        for k, s in enumerate(ss):
            ins = mm(accbank[rows.index(r)], z_src(s), p_src(s), False, k == len(ss) - 1)
        ins.then_inc(T.sem["mm%d" % r], 1)
        minus(cols(T.ysb, r), ext(r, 0), accbank[rows.index(r)], "mm%d" % r, "vy%d" % r)
        y_own = (cols(T.ysb, r), "vy%d" % r, 1)

    u = unit[r]
    for dests, mask in P["p_calls"][r]:
        for m in u:
            need("g", "vp%d" % m, 1)
        send(cols(T.pb, u[0], len(u)), lambda d: cols(T.pb, u[0], len(u)), dests, mask, "pa%d" % u[0])
    for dests, mask in P["y_calls"][r]:
        yu = P["yunit"][r]
        for m in yu:
            need("g", "vy%d" % m, 1)
        send(cols(T.ysb, yu[0], len(yu)), lambda d: cols(T.ysb, yu[0], len(yu)), dests, mask, "ya%d" % yu[0])
    if sent[0]:
        g.wait_ge(T.sem.sent, sent[0])

    need("s", y_own[1], y_own[2])
    g.sync.dma_start(T.y[:, :], y_own[0]).then_inc(T.sem.st, 16)
    g.sync.wait_ge(T.sem.st, 16)
